import numpy as np
import ml_dtypes


def mxq(x, axis, fmt="e4m3"):
    dtype, down = {"e4m3": (ml_dtypes.float8_e4m3fn, 7), "e5m2": (ml_dtypes.float8_e5m2, 14)}[fmt]
    v = np.moveaxis(np.asarray(x, np.float32).astype(ml_dtypes.bfloat16).astype(np.float64), axis, -1)
    blocks = v.reshape(v.shape[:-1] + (-1, 32))
    amax = np.abs(blocks).max(-1, keepdims=True)
    byte = np.maximum(np.where(amax > 0, np.frexp(amax)[1] - 1 + 127, 0) - down, 1)
    scale = np.exp2(byte - 127.0)
    codes = (blocks / scale).astype(np.float32).astype(dtype).astype(np.float64)
    return np.moveaxis((codes * scale).reshape(v.shape), -1, axis)


WIDE = False


def mx_kscale(k):
    if not WIDE:
        return np.ones(k)
    levels = np.array([10, -10, 5, -5, 0])
    if k % 512:
        return np.exp2(np.random.permutation(np.resize(levels, k // 32))).repeat(32)
    a = np.empty((k // 512, 16))
    for p in range(k // 512):
        a[p, :8] = np.random.permutation(np.resize(levels, 8))
        for g in range(8):
            far = levels[np.abs(levels - a[p, g]) >= 10]
            a[p, g + 8] = far[np.random.randint(len(far))]
    return np.exp2(a.ravel()).repeat(32)


def f64(x):
    return np.asarray(x).astype(np.float64)


def striped(idx):
    return np.tile(idx.reshape(-1, 16).T, (8, 1)).astype(np.uint16)


def unstriped(offs):
    return offs[:16].T.reshape(-1).astype(np.int64)


def striped8(idx):
    return np.concatenate([x.reshape(-1, 16).T for x in idx]).astype(np.uint16)


def runs(offs, k):
    lists = np.stack([offs[16 * r : 16 * r + 16].T.reshape(-1) for r in range(8)]).astype(np.int64)
    return lists[np.arange(k) % 512 // 64]


def pack_weight(w):
    k, n = w.shape
    w = f64(np.asarray(w, np.float32).astype(ml_dtypes.bfloat16)).reshape(k // 32, 32, n)
    amax = np.abs(w).max(1)
    byte = np.clip(np.where(amax > 0, np.frexp(amax)[1] - 1 + 127 - 7, 1), 1, 254)
    scaled = (w * np.exp2(127.0 - byte)[:, None, :]).reshape(k, n).astype(np.float32)
    words = np.ascontiguousarray(scaled.reshape(k // 512, 128, 4, n).transpose(0, 1, 3, 2)).astype(ml_dtypes.float8_e4m3fn).view(np.uint8)
    return words, np.ascontiguousarray(byte.astype(np.uint8).reshape(k // 512, 16, n))


def unpack_weight(words, scales):
    g, p, n, _ = words.shape
    vals = np.ascontiguousarray(words).view(ml_dtypes.float8_e4m3fn).astype(np.float64) * np.repeat(np.exp2(scales.astype(np.float64) - 127.0), 8, axis=1)[..., None]
    return vals.transpose(0, 1, 3, 2).reshape(g * 512, n)


K, T, S, N, G, H = 512, 2048, 512, 512, 2048, 512


def setup_inputs():
    n = np.random.standard_normal
    s = mx_kscale(K)[:, None]
    u = mx_kscale(S)
    packed_xT = pack_weight(n((K, T)) * s)
    packed_dT = pack_weight(n((K, G)) / s)
    return {
        "x_words": packed_xT[0],
        "x_scales": packed_xT[1],
        "d_words": packed_dT[0],
        "d_scales": packed_dT[1],
        "gn": (np.random.uniform(0.5, 1.5, (H, 1)) * u[:, None]).astype(np.float32),
        "w1": (n((H, N)) / np.sqrt(H) / u[:, None]).astype(np.float32),
        "offs": striped8(np.random.randint(0, T, (8, S))),
        "k1": striped8(np.random.randint(0, G, (8, H))),
        "n1": striped(np.random.randint(0, S, G)),
        "n2": striped(np.random.permutation(S)),
        "n3": striped(np.random.permutation(S)),
    }


def reference(x_words, x_scales, d_words, d_scales, gn, w1, offs, k1, n1, n2, n3):
    d_k1 = unpack_weight(d_words, d_scales)[np.arange(K)[:, None], runs(k1, K)]
    xq = unpack_weight(x_words, x_scales)[np.arange(K)[:, None], runs(offs, K)]
    h = 0.0625 * (d_k1.T @ xq)
    mb = h[:, unstriped(n1)]
    mx = mb.reshape(H, S, 4).max(axis=2)
    mn = mb.reshape(H, S, 4).min(axis=2)
    z = f64(gn) * (mx - (0.5 * mn))
    h2 = mxq(f64(w1), 0, "e4m3").T @ mxq(z, 0, "e4m3")
    return h2[:, unstriped(n2)] - h2[:, unstriped(n3)]

@@ -1,0 +1,225 @@
+from contextlib import ExitStack
+
+import concourse.mybir as mybir
+
+F32 = mybir.dt.float32
+BF16 = mybir.dt.bfloat16
+I32 = mybir.dt.int32
+U32 = mybir.dt.uint32
+U16 = mybir.dt.uint16
+U8 = mybir.dt.uint8
+FP8X4 = mybir.dt.float8_e4m3fn_x4
+ALU = mybir.AluOpType
+COPY = mybir.ActivationFunctionType.Copy
+
+P = 128
+T = 2048
+S = 512
+H = 512
+N = 512
+PACK = 4
+MEMBERS = 4
+LANES = 16
+CHUNKS = 4
+CJ = S // CHUNKS
+CE = CJ * MEMBERS
+SPARE = 16
+HALF = 256
+
+FLOPS = 2 * 512 * H * S + 2 * H * N * S
+
+
+def tile_picked_hpqgspangap_none_p_kernel(tc, x_words, x_scales, d_words, d_scales, gn, w1, offs, k1, n1, n2, n3, out):
+    nc = tc.nc
+    with ExitStack() as ctx:
+        keep = ctx.enter_context(tc.tile_pool(name="keep", bufs=1))
+        psum = ctx.enter_context(tc.psum_pool(name="psum", bufs=1))
+
+        def new(shape, dtype, name):
+            return keep.tile(shape, dtype, name=name, align_bytes=64)
+
+        def load_list(src, name):
+            tile = new(list(src.shape), U16, name)
+            nc.sync.dma_start(tile[:], src)
+            return tile
+
+        def load_scales(src, name):
+            tile = new([P, T], U8, name)
+            rows = src[0].bitcast(I32).rearrange("q (a c) -> q a c", a=1).to_broadcast([16, 8, T // 4])
+            nc.sync.dma_start(tile[:].bitcast(I32), rows)
+            return tile
+
+        def load_words(src, name):
+            tile = new([P, T], U32, name)
+            nc.sync.dma_start(tile[:].bitcast(I32), src[0].rearrange("p n r -> p (n r)").bitcast(I32))
+            return tile
+
+        k1_sb = load_list(k1, "k1_sb")
+        d_scale_table = load_scales(d_scales, "d_scale_table")
+        offs_sb = load_list(offs, "offs_sb")
+        x_scale_table = load_scales(x_scales, "x_scale_table")
+        d_word_table = load_words(d_words, "d_word_table")
+        x_word_table = load_words(x_words, "x_word_table")
+        n1_sb = load_list(n1, "n1_sb")
+        w_raw = new([P, PACK, N], F32, "w_raw")
+        nc.sync.dma_start(w_raw[:], w1.rearrange("(p t) m -> p t m", t=PACK))
+        n2_sb = load_list(n2, "n2_sb")
+        n3_sb = load_list(n3, "n3_sb")
+        gain_raw = new([P, PACK], F32, "gain_raw")
+        nc.gpsimd.dma_start(gain_raw[:], gn.rearrange("(p t) o -> p (t o)", t=PACK))
+        gain = new([P, PACK], F32, "gain")
+        nc.scalar.activation(gain[:], gain_raw[:], COPY, scale=0.0625)
+
+        h_rows = [new([P, S + SPARE], F32, "h_rows%d" % t) for t in range(PACK)]
+        for t in range(PACK):
+            nc.gpsimd.memset(h_rows[t][:, S:], 0.0)
+
+        picked_scales = new([P, H + S], U8, "picked_scales")
+        nc.vector.tensor_copy(picked_scales[:, :H], d_scale_table[:].indirect(k1_sb[:]))
+        nc.vector.tensor_copy(picked_scales[:, H:], x_scale_table[:].indirect(offs_sb[:]))
+        placed_scales = new([P, H + S], U8, "placed_scales")
+        nc.vector.tensor_copy(placed_scales[:].bitcast(I32), picked_scales[:].bitcast(I32))
+        for i in range(1, 4):
+            nc.scalar.dma_start(placed_scales[i:P:32, :].bitcast(I32), picked_scales[8 * i:P:32, :].bitcast(I32))
+
+        d_picked = new([P, H], U32, "d_picked")
+        nc.vector.tensor_copy(d_picked[:], d_word_table[:].indirect(k1_sb[:]))
+        d_codes = new([P, H], U32, "d_codes")
+        nc.vector.tensor_copy(
+            d_codes[:].rearrange("p (t c i) -> p c t i", t=PACK, i=4),
+            d_picked[:].rearrange("p (c i t) -> p c t i", t=PACK, i=4))
+        d_plane = new([P, H], U8, "d_plane")
+        nc.vector.tensor_copy(
+            d_plane[:].rearrange("p (t m) -> p t m", t=PACK),
+            placed_scales[:, :H].rearrange("p (m t) -> p t m", t=PACK))
+
+        x_codes = new([P, S], U32, "x_codes")
+        for u in range(2):
+            nc.vector.tensor_copy(
+                x_codes[:, u * HALF:(u + 1) * HALF],
+                x_word_table[:].indirect(offs_sb[:, u * HALF // LANES:(u + 1) * HALF // LANES]))
+
+        h_banks = [psum.tile([P, S], F32, name="h_bank%d" % t, tag="first%d" % t) for t in range(PACK)]
+        for u in range(2):
+            for t in range(PACK):
+                nc.tensor.matmul_mx(
+                    out=h_banks[t][:, u * HALF:(u + 1) * HALF],
+                    lhsT=d_codes[:, t * P:(t + 1) * P].bitcast(FP8X4),
+                    lhsT_scale=d_plane[:, t * P:(t + 1) * P],
+                    rhs=x_codes[:, u * HALF:(u + 1) * HALF].bitcast(FP8X4),
+                    rhs_scale=placed_scales[:, H + u * HALF:H + (u + 1) * HALF],
+                    start=True, stop=True)
+
+        w_grouped = new([P, N, PACK], BF16, "w_grouped")
+        nc.gpsimd.tensor_scalar(w_grouped[:], w_raw[:].rearrange("p t m -> p m t"), 1.0, 0.0, ALU.mult, ALU.add)
+        w_codes = new([P, N], U32, "w_codes")
+        w_plane = new([P, N], U8, "w_plane")
+
+        units = [(c, pair) for c in range(CHUNKS) for pair in range(2)]
+        members = {}
+        spans = [new([P, PACK, CJ], F32, "span%d" % c) for c in range(CHUNKS)]
+        h2_banks = [psum.tile([P, S - CJ], F32, name="h2_bank%d" % m) for m in range(4)]
+        h2_rows = [new([P, S], F32, "h2_rows%d" % m) for m in range(4)]
+
+        def gather_members(c, t):
+            key = (c, t // 2)
+            if key not in members:
+                members.setdefault(key, new([P, 2 * CE], F32, "members%d_%d" % key))
+            dst = members[key][:, (t % 2) * CE:(t % 2 + 1) * CE]
+            src = h_rows[t][:].indirect(n1_sb[:, c * CE // LANES:(c + 1) * CE // LANES])
+            if (c, t) == (0, 1):
+                nc.vector.tensor_copy(dst, src)
+            else:
+                nc.scalar.activation(dst, src, COPY)
+
+        def of_pairs(key, op, name):
+            res = new([P, 2 * CJ, 2], F32, "%s%d_%d" % (name, key[0], key[1]))
+            m4 = members[key][:].rearrange("p (g e) -> p g e", e=MEMBERS)
+            nc.vector.tensor_tensor(res[:], m4[:, :, 0:2], m4[:, :, 2:4], op)
+            return res
+
+        def of_two(key, pairs, op, name):
+            res = new([P, 2 * CJ], F32, "%s%d_%d" % (name, key[0], key[1]))
+            nc.vector.tensor_tensor(res[:], pairs[:, :, 0], pairs[:, :, 1], op)
+            return res
+
+        def combine(key, largest, smallest):
+            c, pair = key
+            nc.vector.scalar_tensor_tensor(
+                spans[c][:, 2 * pair:2 * pair + 2, :].rearrange("p t j -> p (t j)"),
+                smallest[:], -0.5, largest[:], ALU.mult, ALU.add)
+
+        def scale_and_round(c):
+            z = new([P, CJ * PACK], BF16, "z%d" % c)
+            nc.vector.tensor_tensor(
+                z[:].rearrange("p (c i t) -> p c t i", t=PACK, i=4),
+                spans[c][:].rearrange("p t (c i) -> p c t i", i=4),
+                gain[:].rearrange("p (c t i) -> p c t i", c=1, i=1).to_broadcast([P, CJ // 4, PACK, 4]),
+                ALU.mult)
+            return z
+
+        def quantise_and_multiply(c, z):
+            z_codes = new([P, CJ], U32, "z_codes%d" % c)
+            z_plane = new([P, CJ], U8, "z_plane%d" % c)
+            nc.vector.quantize_mx(out=z_codes[:].bitcast(FP8X4), scales=z_plane[:], in_=z[:])
+            dsts = []
+            for m in range(4):
+                if c < CHUNKS - 1:
+                    dst = h2_banks[m][:, c * CJ:(c + 1) * CJ]
+                else:
+                    last = psum.tile([P, CJ], F32, name="h2_last%d" % m, tag="first%d" % m)
+                    dst = last[:]
+                nc.tensor.matmul_mx(
+                    out=dst,
+                    lhsT=w_codes[:, m * P:(m + 1) * P].bitcast(FP8X4),
+                    lhsT_scale=w_plane[:, m * P:(m + 1) * P],
+                    rhs=z_codes[:].bitcast(FP8X4), rhs_scale=z_plane[:],
+                    start=True, stop=True)
+                dsts.append(dst)
+            return dsts
+
+        for t in range(PACK):
+            if t == 1:
+                nc.vector.tensor_copy(h_rows[t][:, :S], h_banks[t][:])
+            else:
+                nc.scalar.copy(h_rows[t][:, :S], h_banks[t][:])
+            gather_members(0, t)
+        for c in range(1, CHUNKS):
+            for t in range(PACK):
+                gather_members(c, t)
+
+        before = None
+        for key in units:
+            hi2 = of_pairs(key, ALU.max, "hi2_")
+            lo2 = of_pairs(key, ALU.min, "lo2_")
+            if before is not None:
+                combine(*before)
+            if key == (0, 1):
+                nc.vector.quantize_mx(out=w_codes[:].bitcast(FP8X4), scales=w_plane[:],
+                                      in_=w_grouped[:].rearrange("p m t -> p (m t)"))
+            done = before is not None and before[0][1] == 1
+            largest = of_two(key, hi2, ALU.max, "hi_")
+            if done:
+                z = scale_and_round(before[0][0])
+            smallest = of_two(key, lo2, ALU.min, "lo_")
+            if done:
+                quantise_and_multiply(before[0][0], z)
+            before = (key, largest, smallest)
+        for m in range(4):
+            nc.scalar.copy(h2_rows[m][:, :S - CJ], h2_banks[m][:])
+        combine(*before)
+        lasts = quantise_and_multiply(CHUNKS - 1, scale_and_round(CHUNKS - 1))
+        for m in range(4):
+            if m == 0:
+                nc.scalar.copy(h2_rows[m][:, S - CJ:], lasts[m])
+            else:
+                nc.vector.tensor_copy(h2_rows[m][:, S - CJ:], lasts[m])
+
+        for m in range(4):
+            for u in range(2):
+                cols = slice(u * HALF // LANES, (u + 1) * HALF // LANES)
+                second = new([P, HALF], F32, "second%d_%d" % (m, u))
+                nc.scalar.activation(second[:], h2_rows[m][:].indirect(n3_sb[:, cols]), COPY)
+                gap = new([P, HALF], F32, "gap%d_%d" % (m, u))
+                nc.vector.tensor_tensor(gap[:], h2_rows[m][:].indirect(n2_sb[:, cols]), second[:], ALU.subtract)
+                nc.sync.dma_start(out[m * P:(m + 1) * P, u * HALF:(u + 1) * HALF], gap[:])

@@ -35,8 +35,8 @@ def tile_picked_hpqgspangap_none_p_kernel(tc, x_words, x_scales, d_words, d_scal
         keep = ctx.enter_context(tc.tile_pool(name="keep", bufs=1))
         psum = ctx.enter_context(tc.psum_pool(name="psum", bufs=1))
 
-        def new(shape, dtype, name):
-            return keep.tile(shape, dtype, name=name, align_bytes=64)
+        def new(shape, dtype, name, tag=""):
+            return keep.tile(shape, dtype, name=name, tag=tag, align_bytes=64)
 
         def load_list(src, name):
             tile = new(list(src.shape), U16, name)
@@ -49,8 +49,8 @@ def tile_picked_hpqgspangap_none_p_kernel(tc, x_words, x_scales, d_words, d_scal
             nc.sync.dma_start(tile[:].bitcast(I32), rows)
             return tile
 
-        def load_words(src, name):
-            tile = new([P, T], U32, name)
+        def load_words(src, name, tag=""):
+            tile = new([P, T], U32, name, tag)
             nc.sync.dma_start(tile[:].bitcast(I32), src[0].rearrange("p n r -> p (n r)").bitcast(I32))
             return tile
 
@@ -58,15 +58,13 @@ def tile_picked_hpqgspangap_none_p_kernel(tc, x_words, x_scales, d_words, d_scal
         d_scale_table = load_scales(d_scales, "d_scale_table")
         offs_sb = load_list(offs, "offs_sb")
         x_scale_table = load_scales(x_scales, "x_scale_table")
-        d_word_table = load_words(d_words, "d_word_table")
+        d_word_table = load_words(d_words, "d_word_table", "staging")
         x_word_table = load_words(x_words, "x_word_table")
         n1_sb = load_list(n1, "n1_sb")
-        w_raw = new([P, PACK, N], F32, "w_raw")
-        nc.sync.dma_start(w_raw[:], w1.rearrange("(p t) m -> p t m", t=PACK))
         n2_sb = load_list(n2, "n2_sb")
         n3_sb = load_list(n3, "n3_sb")
         gain_raw = new([P, PACK], F32, "gain_raw")
-        nc.gpsimd.dma_start(gain_raw[:], gn.rearrange("(p t) o -> p (t o)", t=PACK))
+        nc.scalar.dma_start(gain_raw[:], gn.rearrange("(p t) o -> p (t o)", t=PACK))
         gain = new([P, PACK], F32, "gain")
         nc.scalar.activation(gain[:], gain_raw[:], COPY, scale=0.0625)
 
@@ -84,6 +82,8 @@ def tile_picked_hpqgspangap_none_p_kernel(tc, x_words, x_scales, d_words, d_scal
 
         d_picked = new([P, H], U32, "d_picked")
         nc.vector.tensor_copy(d_picked[:], d_word_table[:].indirect(k1_sb[:]))
+        w_raw = new([P, PACK, N], F32, "w_raw", tag="staging")
+        nc.sync.dma_start(w_raw[:], w1.rearrange("(p t) m -> p t m", t=PACK))
         d_codes = new([P, H], U32, "d_codes")
         nc.vector.tensor_copy(
             d_codes[:].rearrange("p (t c i) -> p c t i", t=PACK, i=4),
@@ -111,42 +111,38 @@ def tile_picked_hpqgspangap_none_p_kernel(tc, x_words, x_scales, d_words, d_scal
                     start=True, stop=True)
 
         w_grouped = new([P, N, PACK], BF16, "w_grouped")
-        nc.gpsimd.tensor_scalar(w_grouped[:], w_raw[:].rearrange("p t m -> p m t"), 1.0, 0.0, ALU.mult, ALU.add)
         w_codes = new([P, N], U32, "w_codes")
         w_plane = new([P, N], U8, "w_plane")
 
-        units = [(c, pair) for c in range(CHUNKS) for pair in range(2)]
-        members = {}
+        units = [(c, t0, 2) for c in range(CHUNKS - 1) for t0 in (0, 2)]
+        units = units + [(CHUNKS - 1, 0, 2), (CHUNKS - 1, 2, 1), (CHUNKS - 1, 3, 1)]
+        members = {key: new([P, key[2] * CE], F32, "members%d_%d" % key[:2]) for key in units}
         spans = [new([P, PACK, CJ], F32, "span%d" % c) for c in range(CHUNKS)]
         h2_banks = [psum.tile([P, S - CJ], F32, name="h2_bank%d" % m) for m in range(4)]
         h2_rows = [new([P, S], F32, "h2_rows%d" % m) for m in range(4)]
 
-        def gather_members(c, t):
-            key = (c, t // 2)
-            if key not in members:
-                members.setdefault(key, new([P, 2 * CE], F32, "members%d_%d" % key))
-            dst = members[key][:, (t % 2) * CE:(t % 2 + 1) * CE]
-            src = h_rows[t][:].indirect(n1_sb[:, c * CE // LANES:(c + 1) * CE // LANES])
-            if (c, t) == (0, 1):
-                nc.vector.tensor_copy(dst, src)
-            else:
-                nc.scalar.activation(dst, src, COPY)
+        def gather_members(key):
+            c, t0, width = key
+            for k in range(width):
+                src = h_rows[t0 + k][:].indirect(n1_sb[:, c * CE // LANES:(c + 1) * CE // LANES])
+                nc.scalar.activation(members[key][:, k * CE:(k + 1) * CE], src, COPY)
 
         def of_pairs(key, op, name):
-            res = new([P, 2 * CJ, 2], F32, "%s%d_%d" % (name, key[0], key[1]))
+            res = new([P, key[2] * CJ, 2], F32, "%s%d_%d" % (name, key[0], key[1]),
+                      "staging" if key == units[0] and op == ALU.max else "")
             m4 = members[key][:].rearrange("p (g e) -> p g e", e=MEMBERS)
             nc.vector.tensor_tensor(res[:], m4[:, :, 0:2], m4[:, :, 2:4], op)
             return res
 
         def of_two(key, pairs, op, name):
-            res = new([P, 2 * CJ], F32, "%s%d_%d" % (name, key[0], key[1]))
+            res = new([P, key[2] * CJ], F32, "%s%d_%d" % (name, key[0], key[1]))
             nc.vector.tensor_tensor(res[:], pairs[:, :, 0], pairs[:, :, 1], op)
             return res
 
         def combine(key, largest, smallest):
-            c, pair = key
+            c, t0, width = key
             nc.vector.scalar_tensor_tensor(
-                spans[c][:, 2 * pair:2 * pair + 2, :].rearrange("p t j -> p (t j)"),
+                spans[c][:, t0:t0 + width, :].rearrange("p t j -> p (t j)"),
                 smallest[:], -0.5, largest[:], ALU.mult, ALU.add)
 
         def scale_and_round(c):
@@ -178,15 +174,15 @@ def tile_picked_hpqgspangap_none_p_kernel(tc, x_words, x_scales, d_words, d_scal
                 dsts.append(dst)
             return dsts
 
-        for t in range(PACK):
-            if t == 1:
-                nc.vector.tensor_copy(h_rows[t][:, :S], h_banks[t][:])
-            else:
-                nc.scalar.copy(h_rows[t][:, :S], h_banks[t][:])
-            gather_members(0, t)
-        for c in range(1, CHUNKS):
-            for t in range(PACK):
-                gather_members(c, t)
+        nc.scalar.copy(h_rows[0][:, :S], h_banks[0][:])
+        nc.vector.tensor_copy(h_rows[1][:, :S], h_banks[1][:])
+        nc.vector.tensor_copy(h_rows[2][:, :S], h_banks[2][:])
+        nc.vector.tensor_copy(
+            w_grouped[:].rearrange("p (c i) t -> p c t i", i=4), w_raw[:].rearrange("p t (c i) -> p c t i", i=4))
+        gather_members(units[0])
+        nc.scalar.copy(h_rows[3][:, :S], h_banks[3][:])
+        for key in units[1:]:
+            gather_members(key)
 
         before = None
         for key in units:
@@ -194,10 +190,10 @@ def tile_picked_hpqgspangap_none_p_kernel(tc, x_words, x_scales, d_words, d_scal
             lo2 = of_pairs(key, ALU.min, "lo2_")
             if before is not None:
                 combine(*before)
-            if key == (0, 1):
+            if key == units[0]:
                 nc.vector.quantize_mx(out=w_codes[:].bitcast(FP8X4), scales=w_plane[:],
                                       in_=w_grouped[:].rearrange("p m t -> p (m t)"))
-            done = before is not None and before[0][1] == 1
+            done = before is not None and before[0][1] + before[0][2] == PACK
             largest = of_two(key, hi2, ALU.max, "hi_")
             if done:
                 z = scale_and_round(before[0][0])

@@ -72,26 +72,31 @@ def tile_picked_hpqgspangap_none_p_kernel(tc, x_words, x_scales, d_words, d_scal
         for t in range(PACK):
             nc.gpsimd.memset(h_rows[t][:, S:], 0.0)
 
+        placed_scales = new([P, H + S], U8, "placed_scales")
+        nc.gpsimd.memset(placed_scales[:].bitcast(I32), 0)
         picked_scales = new([P, H + S], U8, "picked_scales")
+        dealt_scales = new([P, H + S], U8, "dealt_scales")
         nc.vector.tensor_copy(picked_scales[:, :H], d_scale_table[:].indirect(k1_sb[:]))
         nc.vector.tensor_copy(picked_scales[:, H:], x_scale_table[:].indirect(offs_sb[:]))
-        placed_scales = new([P, H + S], U8, "placed_scales")
-        nc.vector.tensor_copy(placed_scales[:].bitcast(I32), picked_scales[:].bitcast(I32))
-        for i in range(1, 4):
-            nc.scalar.dma_start(placed_scales[i:P:32, :].bitcast(I32), picked_scales[8 * i:P:32, :].bitcast(I32))
+        nc.vector.tensor_copy(
+            dealt_scales[:, :H].rearrange("p (t m) -> p t m", t=PACK),
+            picked_scales[:, :H].rearrange("p (m t) -> p t m", t=PACK))
+        nc.vector.tensor_copy(dealt_scales[:, H:].bitcast(I32), picked_scales[:, H:].bitcast(I32))
+        for i in range(4):
+            queue = nc.scalar if i % 2 == 0 else nc.sync
+            queue.dma_start(placed_scales[i:P:32, :].bitcast(I32), dealt_scales[8 * i:P:32, :].bitcast(I32))
 
         d_picked = new([P, H], U32, "d_picked")
         nc.vector.tensor_copy(d_picked[:], d_word_table[:].indirect(k1_sb[:]))
-        w_raw = new([P, PACK, N], F32, "w_raw", tag="staging")
-        nc.sync.dma_start(w_raw[:], w1.rearrange("(p t) m -> p t m", t=PACK))
+        w_raw = new([P, PACK * N], F32, "w_raw", tag="staging")
+        w_halves = [w_raw[:, u * PACK * HALF:(u + 1) * PACK * HALF] for u in range(2)]
+        for u in range(2):
+            nc.sync.dma_start(w_halves[u].rearrange("p (t m) -> p t m", t=PACK),
+                              w1[:, u * HALF:(u + 1) * HALF].rearrange("(p t) m -> p t m", t=PACK))
         d_codes = new([P, H], U32, "d_codes")
         nc.vector.tensor_copy(
-            d_codes[:].rearrange("p (t c i) -> p c t i", t=PACK, i=4),
-            d_picked[:].rearrange("p (c i t) -> p c t i", t=PACK, i=4))
-        d_plane = new([P, H], U8, "d_plane")
-        nc.vector.tensor_copy(
-            d_plane[:].rearrange("p (t m) -> p t m", t=PACK),
-            placed_scales[:, :H].rearrange("p (m t) -> p t m", t=PACK))
+            d_codes[:].rearrange("p (a b c i) -> p c a i b", a=2, b=2, i=4),
+            d_picked[:].rearrange("p (c i a b) -> p c a i b", a=2, b=2, i=4))
 
         x_codes = new([P, S], U32, "x_codes")
         for u in range(2):
@@ -100,19 +105,23 @@ def tile_picked_hpqgspangap_none_p_kernel(tc, x_words, x_scales, d_words, d_scal
                 x_word_table[:].indirect(offs_sb[:, u * HALF // LANES:(u + 1) * HALF // LANES]))
 
         h_banks = [psum.tile([P, S], F32, name="h_bank%d" % t, tag="first%d" % t) for t in range(PACK)]
-        for u in range(2):
-            for t in range(PACK):
+        for t in range(PACK):
+            for u in range(2):
                 nc.tensor.matmul_mx(
                     out=h_banks[t][:, u * HALF:(u + 1) * HALF],
                     lhsT=d_codes[:, t * P:(t + 1) * P].bitcast(FP8X4),
-                    lhsT_scale=d_plane[:, t * P:(t + 1) * P],
+                    lhsT_scale=placed_scales[:, t * P:(t + 1) * P],
                     rhs=x_codes[:, u * HALF:(u + 1) * HALF].bitcast(FP8X4),
                     rhs_scale=placed_scales[:, H + u * HALF:H + (u + 1) * HALF],
                     start=True, stop=True)
 
-        w_grouped = new([P, N, PACK], BF16, "w_grouped")
+        w_grouped = new([P, N * PACK], BF16, "w_grouped")
+        for u, move in enumerate((nc.scalar.copy, nc.vector.tensor_copy)):
+            move(w_grouped[:, u * PACK * HALF:(u + 1) * PACK * HALF].rearrange("p (c i t) -> p c t i", t=PACK, i=2),
+                 w_halves[u].rearrange("p (t c i) -> p c t i", t=PACK, i=2))
         w_codes = new([P, N], U32, "w_codes")
         w_plane = new([P, N], U8, "w_plane")
+        nc.vector.quantize_mx(out=w_codes[:].bitcast(FP8X4), scales=w_plane[:], in_=w_grouped[:])
 
         units = [(c, t0, 2) for c in range(CHUNKS - 1) for t0 in (0, 2)]
         units = units + [(CHUNKS - 1, 0, 2), (CHUNKS - 1, 2, 1), (CHUNKS - 1, 3, 1)]
@@ -125,18 +134,21 @@ def tile_picked_hpqgspangap_none_p_kernel(tc, x_words, x_scales, d_words, d_scal
             c, t0, width = key
             for k in range(width):
                 src = h_rows[t0 + k][:].indirect(n1_sb[:, c * CE // LANES:(c + 1) * CE // LANES])
-                nc.scalar.activation(members[key][:, k * CE:(k + 1) * CE], src, COPY)
+                dst = members[key][:, k * CE:(k + 1) * CE]
+                if (c, t0 + k) == (0, 1):
+                    nc.vector.tensor_copy(dst, src)
+                else:
+                    nc.scalar.activation(dst, src, COPY)
 
         def of_pairs(key, op, name):
-            res = new([P, key[2] * CJ, 2], F32, "%s%d_%d" % (name, key[0], key[1]),
-                      "staging" if key == units[0] and op == ALU.max else "")
-            m4 = members[key][:].rearrange("p (g e) -> p g e", e=MEMBERS)
-            nc.vector.tensor_tensor(res[:], m4[:, :, 0:2], m4[:, :, 2:4], op)
+            res = new([P, key[2] * CJ // 2, 4], F32, "%s%d_%d" % (name, key[0], key[1]))
+            m4 = members[key][:].rearrange("p (g i e) -> p g i e", i=2, e=MEMBERS)
+            nc.vector.tensor_tensor(res[:].rearrange("p g (e i) -> p g i e", i=2), m4[:, :, :, 0:2], m4[:, :, :, 2:4], op)
             return res
 
         def of_two(key, pairs, op, name):
             res = new([P, key[2] * CJ], F32, "%s%d_%d" % (name, key[0], key[1]))
-            nc.vector.tensor_tensor(res[:], pairs[:, :, 0], pairs[:, :, 1], op)
+            nc.vector.tensor_tensor(res[:].rearrange("p (g i) -> p g i", i=2), pairs[:, :, 0:2], pairs[:, :, 2:4], op)
             return res
 
         def combine(key, largest, smallest):
@@ -148,10 +160,19 @@ def tile_picked_hpqgspangap_none_p_kernel(tc, x_words, x_scales, d_words, d_scal
         def scale_and_round(c):
             z = new([P, CJ * PACK], BF16, "z%d" % c)
             nc.vector.tensor_tensor(
-                z[:].rearrange("p (c i t) -> p c t i", t=PACK, i=4),
-                spans[c][:].rearrange("p t (c i) -> p c t i", i=4),
-                gain[:].rearrange("p (c t i) -> p c t i", c=1, i=1).to_broadcast([P, CJ // 4, PACK, 4]),
+                z[:].rearrange("p (c i t) -> p c t i", t=PACK, i=2),
+                spans[c][:].rearrange("p t (c i) -> p c t i", i=2),
+                gain[:].rearrange("p (c t i) -> p c t i", c=1, i=1).to_broadcast([P, CJ // 2, PACK, 2]),
                 ALU.mult)
+            return z
+
+        def scale_and_round_on_scalar(c):
+            planes = new([P, PACK * CJ], BF16, "z_planes%d" % c)
+            for t in range(PACK):
+                nc.scalar.activation(planes[:, t * CJ:(t + 1) * CJ], spans[c][:, t, :], COPY, scale=gain[:, t:t + 1])
+            z = new([P, CJ * PACK], BF16, "z%d" % c)
+            nc.scalar.copy(z[:].rearrange("p (c i t) -> p c t i", t=PACK, i=2),
+                           planes[:].rearrange("p (t c i) -> p c t i", t=PACK, i=2))
             return z
 
         def quantise_and_multiply(c, z):
@@ -177,8 +198,6 @@ def tile_picked_hpqgspangap_none_p_kernel(tc, x_words, x_scales, d_words, d_scal
         nc.scalar.copy(h_rows[0][:, :S], h_banks[0][:])
         nc.vector.tensor_copy(h_rows[1][:, :S], h_banks[1][:])
         nc.vector.tensor_copy(h_rows[2][:, :S], h_banks[2][:])
-        nc.vector.tensor_copy(
-            w_grouped[:].rearrange("p (c i) t -> p c t i", i=4), w_raw[:].rearrange("p t (c i) -> p c t i", i=4))
         gather_members(units[0])
         nc.scalar.copy(h_rows[3][:, :S], h_banks[3][:])
         for key in units[1:]:
@@ -190,10 +209,7 @@ def tile_picked_hpqgspangap_none_p_kernel(tc, x_words, x_scales, d_words, d_scal
             lo2 = of_pairs(key, ALU.min, "lo2_")
             if before is not None:
                 combine(*before)
-            if key == units[0]:
-                nc.vector.quantize_mx(out=w_codes[:].bitcast(FP8X4), scales=w_plane[:],
-                                      in_=w_grouped[:].rearrange("p m t -> p (m t)"))
-            done = before is not None and before[0][1] + before[0][2] == PACK
+            done = before is not None and before[0][1] + before[0][2] == PACK and before[0][0] < CHUNKS - 2
             largest = of_two(key, hi2, ALU.max, "hi_")
             if done:
                 z = scale_and_round(before[0][0])
@@ -201,6 +217,7 @@ def tile_picked_hpqgspangap_none_p_kernel(tc, x_words, x_scales, d_words, d_scal
             if done:
                 quantise_and_multiply(before[0][0], z)
             before = (key, largest, smallest)
+        quantise_and_multiply(CHUNKS - 2, scale_and_round_on_scalar(CHUNKS - 2))
         for m in range(4):
             nc.scalar.copy(h2_rows[m][:, :S - CJ], h2_banks[m][:])
         combine(*before)

@@ -43,10 +43,10 @@ def tile_picked_hpqgspangap_none_p_kernel(tc, x_words, x_scales, d_words, d_scal
             nc.sync.dma_start(tile[:], src)
             return tile
 
-        def load_scales(src, name):
+        def load_scales(src, name, engine):
             tile = new([P, T], U8, name)
-            rows = src[0].bitcast(I32).rearrange("q (a c) -> q a c", a=1).to_broadcast([16, 8, T // 4])
-            nc.sync.dma_start(tile[:].bitcast(I32), rows)
+            engine.memset(tile[:].bitcast(I32), 0)
+            nc.sync.dma_start(tile[0:P:8, :].bitcast(I32), src[0].bitcast(I32))
             return tile
 
         def load_words(src, name, tag=""):
@@ -54,13 +54,20 @@ def tile_picked_hpqgspangap_none_p_kernel(tc, x_words, x_scales, d_words, d_scal
             nc.sync.dma_start(tile[:].bitcast(I32), src[0].rearrange("p n r -> p (n r)").bitcast(I32))
             return tile
 
+        def load_w_half(u, tag):
+            tile = new([P, PACK * HALF], F32, "w_half%d" % u, tag)
+            nc.sync.dma_start(tile[:].rearrange("p (t m) -> p t m", t=PACK),
+                              w1[:, u * HALF:(u + 1) * HALF].rearrange("(p t) m -> p t m", t=PACK))
+            return tile
+
         k1_sb = load_list(k1, "k1_sb")
-        d_scale_table = load_scales(d_scales, "d_scale_table")
         offs_sb = load_list(offs, "offs_sb")
-        x_scale_table = load_scales(x_scales, "x_scale_table")
+        n1_sb = load_list(n1, "n1_sb")
+        d_scale_table = load_scales(d_scales, "d_scale_table", nc.gpsimd)
+        x_scale_table = load_scales(x_scales, "x_scale_table", nc.vector)
         d_word_table = load_words(d_words, "d_word_table", "staging")
         x_word_table = load_words(x_words, "x_word_table")
-        n1_sb = load_list(n1, "n1_sb")
+        w_halves = [load_w_half(0, "")]
         n2_sb = load_list(n2, "n2_sb")
         n3_sb = load_list(n3, "n3_sb")
         gain_raw = new([P, PACK], F32, "gain_raw")
@@ -83,16 +90,11 @@ def tile_picked_hpqgspangap_none_p_kernel(tc, x_words, x_scales, d_words, d_scal
             picked_scales[:, :H].rearrange("p (m t) -> p t m", t=PACK))
         nc.vector.tensor_copy(dealt_scales[:, H:].bitcast(I32), picked_scales[:, H:].bitcast(I32))
         for i in range(4):
-            queue = nc.scalar if i % 2 == 0 else nc.sync
-            queue.dma_start(placed_scales[i:P:32, :].bitcast(I32), dealt_scales[8 * i:P:32, :].bitcast(I32))
+            nc.scalar.dma_start(placed_scales[i:P:32, :].bitcast(I32), dealt_scales[8 * i:P:32, :].bitcast(I32))
 
         d_picked = new([P, H], U32, "d_picked")
         nc.vector.tensor_copy(d_picked[:], d_word_table[:].indirect(k1_sb[:]))
-        w_raw = new([P, PACK * N], F32, "w_raw", tag="staging")
-        w_halves = [w_raw[:, u * PACK * HALF:(u + 1) * PACK * HALF] for u in range(2)]
-        for u in range(2):
-            nc.sync.dma_start(w_halves[u].rearrange("p (t m) -> p t m", t=PACK),
-                              w1[:, u * HALF:(u + 1) * HALF].rearrange("(p t) m -> p t m", t=PACK))
+        w_halves.append(load_w_half(1, "staging"))
         d_codes = new([P, H], U32, "d_codes")
         nc.vector.tensor_copy(
             d_codes[:].rearrange("p (a b c i) -> p c a i b", a=2, b=2, i=4),
@@ -118,7 +120,7 @@ def tile_picked_hpqgspangap_none_p_kernel(tc, x_words, x_scales, d_words, d_scal
         w_grouped = new([P, N * PACK], BF16, "w_grouped")
         for u, move in enumerate((nc.scalar.copy, nc.vector.tensor_copy)):
             move(w_grouped[:, u * PACK * HALF:(u + 1) * PACK * HALF].rearrange("p (c i t) -> p c t i", t=PACK, i=2),
-                 w_halves[u].rearrange("p (t c i) -> p c t i", t=PACK, i=2))
+                 w_halves[u][:].rearrange("p (t c i) -> p c t i", t=PACK, i=2))
         w_codes = new([P, N], U32, "w_codes")
         w_plane = new([P, N], U8, "w_plane")
         nc.vector.quantize_mx(out=w_codes[:].bitcast(FP8X4), scales=w_plane[:], in_=w_grouped[:])
@@ -127,7 +129,7 @@ def tile_picked_hpqgspangap_none_p_kernel(tc, x_words, x_scales, d_words, d_scal
         units = units + [(CHUNKS - 1, 0, 2), (CHUNKS - 1, 2, 1), (CHUNKS - 1, 3, 1)]
         members = {key: new([P, key[2] * CE], F32, "members%d_%d" % key[:2]) for key in units}
         spans = [new([P, PACK, CJ], F32, "span%d" % c) for c in range(CHUNKS)]
-        h2_banks = [psum.tile([P, S - CJ], F32, name="h2_bank%d" % m) for m in range(4)]
+        h2_banks = [psum.tile([P, 2 * CJ], F32, name="h2_bank%d" % m, tag="second%d" % m) for m in range(4)]
         h2_rows = [new([P, S], F32, "h2_rows%d" % m) for m in range(4)]
 
         def gather_members(key):
@@ -141,7 +143,8 @@ def tile_picked_hpqgspangap_none_p_kernel(tc, x_words, x_scales, d_words, d_scal
                     nc.scalar.activation(dst, src, COPY)
 
         def of_pairs(key, op, name):
-            res = new([P, key[2] * CJ // 2, 4], F32, "%s%d_%d" % (name, key[0], key[1]))
+            res = new([P, key[2] * CJ // 2, 4], F32, "%s%d_%d" % (name, key[0], key[1]),
+                      "late" if key == units[-1] and op == ALU.min else "")
             m4 = members[key][:].rearrange("p (g i e) -> p g i e", i=2, e=MEMBERS)
             nc.vector.tensor_tensor(res[:].rearrange("p g (e i) -> p g i e", i=2), m4[:, :, :, 0:2], m4[:, :, :, 2:4], op)
             return res
@@ -176,16 +179,16 @@ def tile_picked_hpqgspangap_none_p_kernel(tc, x_words, x_scales, d_words, d_scal
             return z
 
         def quantise_and_multiply(c, z):
-            z_codes = new([P, CJ], U32, "z_codes%d" % c)
+            z_codes = new([P, CJ], U32, "z_codes%d" % c, "late" if c == CHUNKS - 2 else "")
             z_plane = new([P, CJ], U8, "z_plane%d" % c)
             nc.vector.quantize_mx(out=z_codes[:].bitcast(FP8X4), scales=z_plane[:], in_=z[:])
             dsts = []
             for m in range(4):
-                if c < CHUNKS - 1:
+                if c < 2:
                     dst = h2_banks[m][:, c * CJ:(c + 1) * CJ]
                 else:
-                    last = psum.tile([P, CJ], F32, name="h2_last%d" % m, tag="first%d" % m)
-                    dst = last[:]
+                    bank = psum.tile([P, CJ], F32, name="h2_late%d_%d" % (c, m), tag=("first%d" if c == 2 else "second%d") % m)
+                    dst = bank[:]
                 nc.tensor.matmul_mx(
                     out=dst,
                     lhsT=w_codes[:, m * P:(m + 1) * P].bitcast(FP8X4),
@@ -217,10 +220,13 @@ def tile_picked_hpqgspangap_none_p_kernel(tc, x_words, x_scales, d_words, d_scal
             if done:
                 quantise_and_multiply(before[0][0], z)
             before = (key, largest, smallest)
-        quantise_and_multiply(CHUNKS - 2, scale_and_round_on_scalar(CHUNKS - 2))
+        z = scale_and_round_on_scalar(CHUNKS - 2)
         for m in range(4):
-            nc.scalar.copy(h2_rows[m][:, :S - CJ], h2_banks[m][:])
+            nc.scalar.copy(h2_rows[m][:, :2 * CJ], h2_banks[m][:])
         combine(*before)
+        thirds = quantise_and_multiply(CHUNKS - 2, z)
+        for m in range(4):
+            nc.scalar.copy(h2_rows[m][:, 2 * CJ:3 * CJ], thirds[m])
         lasts = quantise_and_multiply(CHUNKS - 1, scale_and_round(CHUNKS - 1))
         for m in range(4):
             if m == 0:

@@ -13,23 +13,30 @@ ALU = mybir.AluOpType
 COPY = mybir.ActivationFunctionType.Copy
 
 P = 128
+K = 512
 T = 2048
 S = 512
 H = 512
 N = 512
 PACK = 4
+QUADRANT = 32
+BLOCK_ROWS = 8
 MEMBERS = 4
 LANES = 16
+M_TILES = N // P
+HALF = 256
 CHUNKS = 4
 CJ = S // CHUNKS
 CE = CJ * MEMBERS
+LAST = CHUNKS - 1
+EARLY = CHUNKS - 2
 SPARE = 16
-HALF = 256
 
-FLOPS = 2 * 512 * H * S + 2 * H * N * S
+FLOPS = 2 * K * H * S + 2 * H * N * S
 
 
-def tile_picked_hpqgspangap_none_p_kernel(tc, x_words, x_scales, d_words, d_scales, gn, w1, offs, k1, n1, n2, n3, out):
+def tile_picked_hpqgspangap_none_p_kernel(
+        tc, x_words, x_scales, d_words, d_scales, gn, w1, offs, k1, n1, n2, n3, out):
     nc = tc.nc
     with ExitStack() as ctx:
         keep = ctx.enter_context(tc.tile_pool(name="keep", bufs=1))
@@ -37,6 +44,9 @@ def tile_picked_hpqgspangap_none_p_kernel(tc, x_words, x_scales, d_words, d_scal
 
         def new(shape, dtype, name, tag=""):
             return keep.tile(shape, dtype, name=name, tag=tag, align_bytes=64)
+
+        def entries(listed, first, count):
+            return listed[:, first // LANES:(first + count) // LANES]
 
         def load_list(src, name):
             tile = new(list(src.shape), U16, name)
@@ -46,7 +56,7 @@ def tile_picked_hpqgspangap_none_p_kernel(tc, x_words, x_scales, d_words, d_scal
         def load_scales(src, name, engine):
             tile = new([P, T], U8, name)
             engine.memset(tile[:].bitcast(I32), 0)
-            nc.sync.dma_start(tile[0:P:8, :].bitcast(I32), src[0].bitcast(I32))
+            nc.sync.dma_start(tile[0:P:BLOCK_ROWS, :].bitcast(I32), src[0].bitcast(I32))
             return tile
 
         def load_words(src, name, tag=""):
@@ -54,7 +64,7 @@ def tile_picked_hpqgspangap_none_p_kernel(tc, x_words, x_scales, d_words, d_scal
             nc.sync.dma_start(tile[:].bitcast(I32), src[0].rearrange("p n r -> p (n r)").bitcast(I32))
             return tile
 
-        def load_w_half(u, tag):
+        def load_w_half(u, tag=""):
             tile = new([P, PACK * HALF], F32, "w_half%d" % u, tag)
             nc.sync.dma_start(tile[:].rearrange("p (t m) -> p t m", t=PACK),
                               w1[:, u * HALF:(u + 1) * HALF].rearrange("(p t) m -> p t m", t=PACK))
@@ -67,7 +77,7 @@ def tile_picked_hpqgspangap_none_p_kernel(tc, x_words, x_scales, d_words, d_scal
         x_scale_table = load_scales(x_scales, "x_scale_table", nc.vector)
         d_word_table = load_words(d_words, "d_word_table", "staging")
         x_word_table = load_words(x_words, "x_word_table")
-        w_halves = [load_w_half(0, "")]
+        w_halves = [load_w_half(0)]
         n2_sb = load_list(n2, "n2_sb")
         n3_sb = load_list(n3, "n3_sb")
         gain_raw = new([P, PACK], F32, "gain_raw")
@@ -89,8 +99,9 @@ def tile_picked_hpqgspangap_none_p_kernel(tc, x_words, x_scales, d_words, d_scal
             dealt_scales[:, :H].rearrange("p (t m) -> p t m", t=PACK),
             picked_scales[:, :H].rearrange("p (m t) -> p t m", t=PACK))
         nc.vector.tensor_copy(dealt_scales[:, H:].bitcast(I32), picked_scales[:, H:].bitcast(I32))
-        for i in range(4):
-            nc.scalar.dma_start(placed_scales[i:P:32, :].bitcast(I32), dealt_scales[8 * i:P:32, :].bitcast(I32))
+        for i in range(QUADRANT // BLOCK_ROWS):
+            nc.scalar.dma_start(placed_scales[i:P:QUADRANT, :].bitcast(I32),
+                                dealt_scales[BLOCK_ROWS * i:P:QUADRANT, :].bitcast(I32))
 
         d_picked = new([P, H], U32, "d_picked")
         nc.vector.tensor_copy(d_picked[:], d_word_table[:].indirect(k1_sb[:]))
@@ -100,22 +111,22 @@ def tile_picked_hpqgspangap_none_p_kernel(tc, x_words, x_scales, d_words, d_scal
             d_codes[:].rearrange("p (a b c i) -> p c a i b", a=2, b=2, i=4),
             d_picked[:].rearrange("p (c i a b) -> p c a i b", a=2, b=2, i=4))
 
-        x_codes = new([P, S], U32, "x_codes")
+        x_codes = [new([P, HALF], U32, "x_codes%d" % u) for u in range(2)]
         for u in range(2):
-            nc.vector.tensor_copy(
-                x_codes[:, u * HALF:(u + 1) * HALF],
-                x_word_table[:].indirect(offs_sb[:, u * HALF // LANES:(u + 1) * HALF // LANES]))
+            nc.vector.tensor_copy(x_codes[u][:], x_word_table[:].indirect(entries(offs_sb, u * HALF, HALF)))
 
         h_banks = [psum.tile([P, S], F32, name="h_bank%d" % t, tag="first%d" % t) for t in range(PACK)]
+        h_early = psum.tile([P, HALF], F32, name="h_early", tag="second0")
         for t in range(PACK):
             for u in range(2):
                 nc.tensor.matmul_mx(
-                    out=h_banks[t][:, u * HALF:(u + 1) * HALF],
+                    out=h_early[:] if (t, u) == (0, 0) else h_banks[t][:, u * HALF:(u + 1) * HALF],
                     lhsT=d_codes[:, t * P:(t + 1) * P].bitcast(FP8X4),
                     lhsT_scale=placed_scales[:, t * P:(t + 1) * P],
-                    rhs=x_codes[:, u * HALF:(u + 1) * HALF].bitcast(FP8X4),
+                    rhs=x_codes[u][:].bitcast(FP8X4),
                     rhs_scale=placed_scales[:, H + u * HALF:H + (u + 1) * HALF],
                     start=True, stop=True)
+        nc.scalar.copy(h_rows[0][:, :HALF], h_early[:])
 
         w_grouped = new([P, N * PACK], BF16, "w_grouped")
         for u, move in enumerate((nc.scalar.copy, nc.vector.tensor_copy)):
@@ -125,42 +136,42 @@ def tile_picked_hpqgspangap_none_p_kernel(tc, x_words, x_scales, d_words, d_scal
         w_plane = new([P, N], U8, "w_plane")
         nc.vector.quantize_mx(out=w_codes[:].bitcast(FP8X4), scales=w_plane[:], in_=w_grouped[:])
 
-        units = [(c, t0, 2) for c in range(CHUNKS - 1) for t0 in (0, 2)]
-        units = units + [(CHUNKS - 1, 0, 2), (CHUNKS - 1, 2, 1), (CHUNKS - 1, 3, 1)]
-        members = {key: new([P, key[2] * CE], F32, "members%d_%d" % key[:2]) for key in units}
+        units = [(c, t0, 2) for c in range(LAST) for t0 in (0, 2)] + [(LAST, 0, 2), (LAST, 2, 1), (LAST, 3, 1)]
+        members = {unit: new([P, unit[2] * CE], F32, "members%d_%d" % unit[:2]) for unit in units}
         spans = [new([P, PACK, CJ], F32, "span%d" % c) for c in range(CHUNKS)]
-        h2_banks = [psum.tile([P, 2 * CJ], F32, name="h2_bank%d" % m, tag="second%d" % m) for m in range(4)]
-        h2_rows = [new([P, S], F32, "h2_rows%d" % m) for m in range(4)]
+        h2_banks = [psum.tile([P, EARLY * CJ], F32, name="h2_bank%d" % m, tag="second%d" % m) for m in range(M_TILES)]
+        h2_rows = [new([P, S], F32, "h2_rows%d" % m) for m in range(M_TILES)]
 
-        def gather_members(key):
-            c, t0, width = key
+        def gather_members(unit):
+            c, t0, width = unit
             for k in range(width):
-                src = h_rows[t0 + k][:].indirect(n1_sb[:, c * CE // LANES:(c + 1) * CE // LANES])
-                dst = members[key][:, k * CE:(k + 1) * CE]
+                src = h_rows[t0 + k][:].indirect(entries(n1_sb, c * CE, CE))
+                dst = members[unit][:, k * CE:(k + 1) * CE]
                 if (c, t0 + k) == (0, 1):
                     nc.vector.tensor_copy(dst, src)
                 else:
                     nc.scalar.activation(dst, src, COPY)
 
-        def of_pairs(key, op, name):
-            res = new([P, key[2] * CJ // 2, 4], F32, "%s%d_%d" % (name, key[0], key[1]),
-                      "late" if key == units[-1] and op == ALU.min else "")
-            m4 = members[key][:].rearrange("p (g i e) -> p g i e", i=2, e=MEMBERS)
-            nc.vector.tensor_tensor(res[:].rearrange("p g (e i) -> p g i e", i=2), m4[:, :, :, 0:2], m4[:, :, :, 2:4], op)
-            return res
+        def of_four(unit, op, name, tag=""):
+            pairs = new([P, unit[2] * CJ // 2, 4], F32, "%s%d_%d" % (name, unit[0], unit[1]), tag)
+            four = members[unit][:].rearrange("p (g i e) -> p g i e", i=2, e=MEMBERS)
+            nc.vector.tensor_tensor(
+                pairs[:].rearrange("p g (e i) -> p g i e", i=2), four[:, :, :, 0:2], four[:, :, :, 2:4], op)
+            return pairs
 
-        def of_two(key, pairs, op, name):
-            res = new([P, key[2] * CJ], F32, "%s%d_%d" % (name, key[0], key[1]))
-            nc.vector.tensor_tensor(res[:].rearrange("p (g i) -> p g i", i=2), pairs[:, :, 0:2], pairs[:, :, 2:4], op)
-            return res
+        def of_two(unit, pairs, op, name):
+            single = new([P, unit[2] * CJ], F32, "%s%d_%d" % (name, unit[0], unit[1]))
+            nc.vector.tensor_tensor(
+                single[:].rearrange("p (g i) -> p g i", i=2), pairs[:, :, 0:2], pairs[:, :, 2:4], op)
+            return single
 
-        def combine(key, largest, smallest):
-            c, t0, width = key
+        def combine(unit, largest, smallest):
+            c, t0, width = unit
             nc.vector.scalar_tensor_tensor(
                 spans[c][:, t0:t0 + width, :].rearrange("p t j -> p (t j)"),
                 smallest[:], -0.5, largest[:], ALU.mult, ALU.add)
 
-        def scale_and_round(c):
+        def round_on_vector(c):
             z = new([P, CJ * PACK], BF16, "z%d" % c)
             nc.vector.tensor_tensor(
                 z[:].rearrange("p (c i t) -> p c t i", t=PACK, i=2),
@@ -169,76 +180,76 @@ def tile_picked_hpqgspangap_none_p_kernel(tc, x_words, x_scales, d_words, d_scal
                 ALU.mult)
             return z
 
-        def scale_and_round_on_scalar(c):
-            planes = new([P, PACK * CJ], BF16, "z_planes%d" % c)
+        def round_on_scalar(c):
+            rounded = new([P, PACK * CJ], BF16, "rounded%d" % c)
             for t in range(PACK):
-                nc.scalar.activation(planes[:, t * CJ:(t + 1) * CJ], spans[c][:, t, :], COPY, scale=gain[:, t:t + 1])
+                nc.scalar.activation(rounded[:, t * CJ:(t + 1) * CJ], spans[c][:, t, :], COPY, scale=gain[:, t:t + 1])
             z = new([P, CJ * PACK], BF16, "z%d" % c)
             nc.scalar.copy(z[:].rearrange("p (c i t) -> p c t i", t=PACK, i=2),
-                           planes[:].rearrange("p (t c i) -> p c t i", t=PACK, i=2))
+                           rounded[:].rearrange("p (t c i) -> p c t i", t=PACK, i=2))
             return z
 
-        def quantise_and_multiply(c, z):
-            z_codes = new([P, CJ], U32, "z_codes%d" % c, "late" if c == CHUNKS - 2 else "")
+        def early_bank(c, m):
+            return h2_banks[m][:, c * CJ:(c + 1) * CJ]
+
+        def reused_bank(tag):
+            return lambda c, m: psum.tile([P, CJ], F32, name="h2_late%d_%d" % (c, m), tag="%s%d" % (tag, m))[:]
+
+        def quantise_and_multiply(c, z, bank_of, tag=""):
+            z_codes = new([P, CJ], U32, "z_codes%d" % c, tag)
             z_plane = new([P, CJ], U8, "z_plane%d" % c)
             nc.vector.quantize_mx(out=z_codes[:].bitcast(FP8X4), scales=z_plane[:], in_=z[:])
-            dsts = []
-            for m in range(4):
-                if c < 2:
-                    dst = h2_banks[m][:, c * CJ:(c + 1) * CJ]
-                else:
-                    bank = psum.tile([P, CJ], F32, name="h2_late%d_%d" % (c, m), tag=("first%d" if c == 2 else "second%d") % m)
-                    dst = bank[:]
+            products = []
+            for m in range(M_TILES):
+                products.append(bank_of(c, m))
                 nc.tensor.matmul_mx(
-                    out=dst,
+                    out=products[m],
                     lhsT=w_codes[:, m * P:(m + 1) * P].bitcast(FP8X4),
                     lhsT_scale=w_plane[:, m * P:(m + 1) * P],
                     rhs=z_codes[:].bitcast(FP8X4), rhs_scale=z_plane[:],
                     start=True, stop=True)
-                dsts.append(dst)
-            return dsts
+            return products
 
-        nc.scalar.copy(h_rows[0][:, :S], h_banks[0][:])
+        nc.scalar.copy(h_rows[0][:, HALF:S], h_banks[0][:, HALF:])
         nc.vector.tensor_copy(h_rows[1][:, :S], h_banks[1][:])
         nc.vector.tensor_copy(h_rows[2][:, :S], h_banks[2][:])
         gather_members(units[0])
-        nc.scalar.copy(h_rows[3][:, :S], h_banks[3][:])
-        for key in units[1:]:
-            gather_members(key)
+        nc.vector.tensor_copy(h_rows[3][:, :S], h_banks[3][:])
+        for unit in units[1:]:
+            gather_members(unit)
 
         before = None
-        for key in units:
-            hi2 = of_pairs(key, ALU.max, "hi2_")
-            lo2 = of_pairs(key, ALU.min, "lo2_")
+        for unit in units:
+            pair_max = of_four(unit, ALU.max, "pair_max")
+            pair_min = of_four(unit, ALU.min, "pair_min", "late" if unit == units[-1] else "")
             if before is not None:
                 combine(*before)
-            done = before is not None and before[0][1] + before[0][2] == PACK and before[0][0] < CHUNKS - 2
-            largest = of_two(key, hi2, ALU.max, "hi_")
-            if done:
-                z = scale_and_round(before[0][0])
-            smallest = of_two(key, lo2, ALU.min, "lo_")
-            if done:
-                quantise_and_multiply(before[0][0], z)
-            before = (key, largest, smallest)
-        z = scale_and_round_on_scalar(CHUNKS - 2)
-        for m in range(4):
-            nc.scalar.copy(h2_rows[m][:, :2 * CJ], h2_banks[m][:])
-        combine(*before)
-        thirds = quantise_and_multiply(CHUNKS - 2, z)
-        for m in range(4):
-            nc.scalar.copy(h2_rows[m][:, 2 * CJ:3 * CJ], thirds[m])
-        lasts = quantise_and_multiply(CHUNKS - 1, scale_and_round(CHUNKS - 1))
-        for m in range(4):
-            if m == 0:
-                nc.scalar.copy(h2_rows[m][:, S - CJ:], lasts[m])
-            else:
-                nc.vector.tensor_copy(h2_rows[m][:, S - CJ:], lasts[m])
+            finish_chunk = unit[1] == 0 and 0 < unit[0] <= EARLY
+            largest = of_two(unit, pair_max, ALU.max, "largest")
+            if finish_chunk:
+                z = round_on_vector(unit[0] - 1)
+            smallest = of_two(unit, pair_min, ALU.min, "smallest")
+            if finish_chunk:
+                quantise_and_multiply(unit[0] - 1, z, early_bank)
+            before = (unit, largest, smallest)
 
-        for m in range(4):
+        z = round_on_scalar(EARLY)
+        for m in range(M_TILES):
+            nc.scalar.copy(h2_rows[m][:, :EARLY * CJ], h2_banks[m][:])
+        combine(*before)
+        products = quantise_and_multiply(EARLY, z, reused_bank("first"), "late")
+        for m in range(M_TILES):
+            nc.scalar.copy(h2_rows[m][:, EARLY * CJ:LAST * CJ], products[m])
+        products = quantise_and_multiply(LAST, round_on_vector(LAST), reused_bank("second"))
+        nc.scalar.copy(h2_rows[0][:, LAST * CJ:], products[0])
+        for m in range(1, M_TILES):
+            nc.vector.tensor_copy(h2_rows[m][:, LAST * CJ:], products[m])
+
+        for m in range(M_TILES):
             for u in range(2):
-                cols = slice(u * HALF // LANES, (u + 1) * HALF // LANES)
-                second = new([P, HALF], F32, "second%d_%d" % (m, u))
-                nc.scalar.activation(second[:], h2_rows[m][:].indirect(n3_sb[:, cols]), COPY)
+                at_n3 = new([P, HALF], F32, "at_n3_%d_%d" % (m, u))
+                nc.scalar.activation(at_n3[:], h2_rows[m][:].indirect(entries(n3_sb, u * HALF, HALF)), COPY)
                 gap = new([P, HALF], F32, "gap%d_%d" % (m, u))
-                nc.vector.tensor_tensor(gap[:], h2_rows[m][:].indirect(n2_sb[:, cols]), second[:], ALU.subtract)
+                nc.vector.tensor_tensor(
+                    gap[:], h2_rows[m][:].indirect(entries(n2_sb, u * HALF, HALF)), at_n3[:], ALU.subtract)
                 nc.sync.dma_start(out[m * P:(m + 1) * P, u * HALF:(u + 1) * HALF], gap[:])

from contextlib import ExitStack

import concourse.mybir as mybir

F32 = mybir.dt.float32
BF16 = mybir.dt.bfloat16
I32 = mybir.dt.int32
U32 = mybir.dt.uint32
U16 = mybir.dt.uint16
U8 = mybir.dt.uint8
FP8X4 = mybir.dt.float8_e4m3fn_x4
ALU = mybir.AluOpType
COPY = mybir.ActivationFunctionType.Copy

P = 128
K = 512
T = 2048
S = 512
H = 512
N = 512
PACK = 4
QUADRANT = 32
BLOCK_ROWS = 8
MEMBERS = 4
LANES = 16
M_TILES = N // P
HALF = 256
CHUNKS = 4
CJ = S // CHUNKS
CE = CJ * MEMBERS
LAST = CHUNKS - 1
EARLY = CHUNKS - 2
SPARE = 16

FLOPS = 2 * K * H * S + 2 * H * N * S


def tile_picked_hpqgspangap_none_p_kernel(
        tc, x_words, x_scales, d_words, d_scales, gn, w1, offs, k1, n1, n2, n3, out):
    nc = tc.nc
    with ExitStack() as ctx:
        keep = ctx.enter_context(tc.tile_pool(name="keep", bufs=1))
        psum = ctx.enter_context(tc.psum_pool(name="psum", bufs=1))

        def new(shape, dtype, name, tag=""):
            return keep.tile(shape, dtype, name=name, tag=tag, align_bytes=64)

        def entries(listed, first, count):
            return listed[:, first // LANES:(first + count) // LANES]

        def load_list(src, name):
            tile = new(list(src.shape), U16, name)
            nc.sync.dma_start(tile[:], src)
            return tile

        def load_scales(src, name, engine):
            tile = new([P, T], U8, name)
            engine.memset(tile[:].bitcast(I32), 0)
            nc.sync.dma_start(tile[0:P:BLOCK_ROWS, :].bitcast(I32), src[0].bitcast(I32))
            return tile

        def load_words(src, name, tag=""):
            tile = new([P, T], U32, name, tag)
            nc.sync.dma_start(tile[:].bitcast(I32), src[0].rearrange("p n r -> p (n r)").bitcast(I32))
            return tile

        def load_w_half(u, tag=""):
            tile = new([P, PACK * HALF], F32, "w_half%d" % u, tag)
            nc.sync.dma_start(tile[:].rearrange("p (t m) -> p t m", t=PACK),
                              w1[:, u * HALF:(u + 1) * HALF].rearrange("(p t) m -> p t m", t=PACK))
            return tile

        k1_sb = load_list(k1, "k1_sb")
        offs_sb = load_list(offs, "offs_sb")
        n1_sb = load_list(n1, "n1_sb")
        d_scale_table = load_scales(d_scales, "d_scale_table", nc.gpsimd)
        x_scale_table = load_scales(x_scales, "x_scale_table", nc.vector)
        d_word_table = load_words(d_words, "d_word_table", "staging")
        x_word_table = load_words(x_words, "x_word_table")
        w_halves = [load_w_half(0)]
        n2_sb = load_list(n2, "n2_sb")
        n3_sb = load_list(n3, "n3_sb")
        gain_raw = new([P, PACK], F32, "gain_raw")
        nc.scalar.dma_start(gain_raw[:], gn.rearrange("(p t) o -> p (t o)", t=PACK))
        gain = new([P, PACK], F32, "gain")
        nc.scalar.activation(gain[:], gain_raw[:], COPY, scale=0.0625)

        h_rows = [new([P, S + SPARE], F32, "h_rows%d" % t) for t in range(PACK)]
        for t in range(PACK):
            nc.gpsimd.memset(h_rows[t][:, S:], 0.0)

        placed_scales = new([P, H + S], U8, "placed_scales")
        nc.gpsimd.memset(placed_scales[:].bitcast(I32), 0)
        picked_scales = new([P, H + S], U8, "picked_scales")
        dealt_scales = new([P, H + S], U8, "dealt_scales")
        nc.vector.tensor_copy(picked_scales[:, :H], d_scale_table[:].indirect(k1_sb[:]))
        nc.vector.tensor_copy(picked_scales[:, H:], x_scale_table[:].indirect(offs_sb[:]))
        nc.vector.tensor_copy(
            dealt_scales[:, :H].rearrange("p (t m) -> p t m", t=PACK),
            picked_scales[:, :H].rearrange("p (m t) -> p t m", t=PACK))
        nc.vector.tensor_copy(dealt_scales[:, H:].bitcast(I32), picked_scales[:, H:].bitcast(I32))
        for i in range(QUADRANT // BLOCK_ROWS):
            nc.scalar.dma_start(placed_scales[i:P:QUADRANT, :].bitcast(I32),
                                dealt_scales[BLOCK_ROWS * i:P:QUADRANT, :].bitcast(I32))

        d_picked = new([P, H], U32, "d_picked")
        nc.vector.tensor_copy(d_picked[:], d_word_table[:].indirect(k1_sb[:]))
        w_halves.append(load_w_half(1, "staging"))
        d_codes = new([P, H], U32, "d_codes")
        nc.vector.tensor_copy(
            d_codes[:].rearrange("p (a b c i) -> p c a i b", a=2, b=2, i=4),
            d_picked[:].rearrange("p (c i a b) -> p c a i b", a=2, b=2, i=4))

        x_codes = [new([P, HALF], U32, "x_codes%d" % u) for u in range(2)]
        for u in range(2):
            nc.vector.tensor_copy(x_codes[u][:], x_word_table[:].indirect(entries(offs_sb, u * HALF, HALF)))

        h_banks = [psum.tile([P, S], F32, name="h_bank%d" % t, tag="first%d" % t) for t in range(PACK)]
        h_early = psum.tile([P, HALF], F32, name="h_early", tag="second0")
        for t in range(PACK):
            for u in range(2):
                nc.tensor.matmul_mx(
                    out=h_early[:] if (t, u) == (0, 0) else h_banks[t][:, u * HALF:(u + 1) * HALF],
                    lhsT=d_codes[:, t * P:(t + 1) * P].bitcast(FP8X4),
                    lhsT_scale=placed_scales[:, t * P:(t + 1) * P],
                    rhs=x_codes[u][:].bitcast(FP8X4),
                    rhs_scale=placed_scales[:, H + u * HALF:H + (u + 1) * HALF],
                    start=True, stop=True)
        nc.scalar.copy(h_rows[0][:, :HALF], h_early[:])

        w_grouped = new([P, N * PACK], BF16, "w_grouped")
        for u, move in enumerate((nc.scalar.copy, nc.vector.tensor_copy)):
            move(w_grouped[:, u * PACK * HALF:(u + 1) * PACK * HALF].rearrange("p (c i t) -> p c t i", t=PACK, i=2),
                 w_halves[u][:].rearrange("p (t c i) -> p c t i", t=PACK, i=2))
        w_codes = new([P, N], U32, "w_codes")
        w_plane = new([P, N], U8, "w_plane")
        nc.vector.quantize_mx(out=w_codes[:].bitcast(FP8X4), scales=w_plane[:], in_=w_grouped[:])

        units = [(c, t0, 2) for c in range(LAST) for t0 in (0, 2)] + [(LAST, 0, 2), (LAST, 2, 1), (LAST, 3, 1)]
        members = {unit: new([P, unit[2] * CE], F32, "members%d_%d" % unit[:2]) for unit in units}
        spans = [new([P, PACK, CJ], F32, "span%d" % c) for c in range(CHUNKS)]
        h2_banks = [psum.tile([P, EARLY * CJ], F32, name="h2_bank%d" % m, tag="second%d" % m) for m in range(M_TILES)]
        h2_rows = [new([P, S], F32, "h2_rows%d" % m) for m in range(M_TILES)]

        def gather_members(unit):
            c, t0, width = unit
            for k in range(width):
                src = h_rows[t0 + k][:].indirect(entries(n1_sb, c * CE, CE))
                dst = members[unit][:, k * CE:(k + 1) * CE]
                if (c, t0 + k) == (0, 1):
                    nc.vector.tensor_copy(dst, src)
                else:
                    nc.scalar.activation(dst, src, COPY)

        def of_four(unit, op, name, tag=""):
            pairs = new([P, unit[2] * CJ // 2, 4], F32, "%s%d_%d" % (name, unit[0], unit[1]), tag)
            four = members[unit][:].rearrange("p (g i e) -> p g i e", i=2, e=MEMBERS)
            nc.vector.tensor_tensor(
                pairs[:].rearrange("p g (e i) -> p g i e", i=2), four[:, :, :, 0:2], four[:, :, :, 2:4], op)
            return pairs

        def of_two(unit, pairs, op, name):
            single = new([P, unit[2] * CJ], F32, "%s%d_%d" % (name, unit[0], unit[1]))
            nc.vector.tensor_tensor(
                single[:].rearrange("p (g i) -> p g i", i=2), pairs[:, :, 0:2], pairs[:, :, 2:4], op)
            return single

        def combine(unit, largest, smallest):
            c, t0, width = unit
            nc.vector.scalar_tensor_tensor(
                spans[c][:, t0:t0 + width, :].rearrange("p t j -> p (t j)"),
                smallest[:], -0.5, largest[:], ALU.mult, ALU.add)

        def round_on_vector(c):
            z = new([P, CJ * PACK], BF16, "z%d" % c)
            nc.vector.tensor_tensor(
                z[:].rearrange("p (c i t) -> p c t i", t=PACK, i=2),
                spans[c][:].rearrange("p t (c i) -> p c t i", i=2),
                gain[:].rearrange("p (c t i) -> p c t i", c=1, i=1).to_broadcast([P, CJ // 2, PACK, 2]),
                ALU.mult)
            return z

        def round_on_scalar(c):
            rounded = new([P, PACK * CJ], BF16, "rounded%d" % c)
            for t in range(PACK):
                nc.scalar.activation(rounded[:, t * CJ:(t + 1) * CJ], spans[c][:, t, :], COPY, scale=gain[:, t:t + 1])
            z = new([P, CJ * PACK], BF16, "z%d" % c)
            nc.scalar.copy(z[:].rearrange("p (c i t) -> p c t i", t=PACK, i=2),
                           rounded[:].rearrange("p (t c i) -> p c t i", t=PACK, i=2))
            return z

        def early_bank(c, m):
            return h2_banks[m][:, c * CJ:(c + 1) * CJ]

        def reused_bank(tag):
            return lambda c, m: psum.tile([P, CJ], F32, name="h2_late%d_%d" % (c, m), tag="%s%d" % (tag, m))[:]

        def quantise_and_multiply(c, z, bank_of, tag=""):
            z_codes = new([P, CJ], U32, "z_codes%d" % c, tag)
            z_plane = new([P, CJ], U8, "z_plane%d" % c)
            nc.vector.quantize_mx(out=z_codes[:].bitcast(FP8X4), scales=z_plane[:], in_=z[:])
            products = []
            for m in range(M_TILES):
                products.append(bank_of(c, m))
                nc.tensor.matmul_mx(
                    out=products[m],
                    lhsT=w_codes[:, m * P:(m + 1) * P].bitcast(FP8X4),
                    lhsT_scale=w_plane[:, m * P:(m + 1) * P],
                    rhs=z_codes[:].bitcast(FP8X4), rhs_scale=z_plane[:],
                    start=True, stop=True)
            return products

        nc.scalar.copy(h_rows[0][:, HALF:S], h_banks[0][:, HALF:])
        nc.vector.tensor_copy(h_rows[1][:, :S], h_banks[1][:])
        nc.vector.tensor_copy(h_rows[2][:, :S], h_banks[2][:])
        gather_members(units[0])
        nc.vector.tensor_copy(h_rows[3][:, :S], h_banks[3][:])
        for unit in units[1:]:
            gather_members(unit)

        before = None
        for unit in units:
            pair_max = of_four(unit, ALU.max, "pair_max")
            pair_min = of_four(unit, ALU.min, "pair_min", "late" if unit == units[-1] else "")
            if before is not None:
                combine(*before)
            finish_chunk = unit[1] == 0 and 0 < unit[0] <= EARLY
            largest = of_two(unit, pair_max, ALU.max, "largest")
            if finish_chunk:
                z = round_on_vector(unit[0] - 1)
            smallest = of_two(unit, pair_min, ALU.min, "smallest")
            if finish_chunk:
                quantise_and_multiply(unit[0] - 1, z, early_bank)
            before = (unit, largest, smallest)

        z = round_on_scalar(EARLY)
        for m in range(M_TILES):
            nc.scalar.copy(h2_rows[m][:, :EARLY * CJ], h2_banks[m][:])
        combine(*before)
        products = quantise_and_multiply(EARLY, z, reused_bank("first"), "late")
        for m in range(M_TILES):
            nc.scalar.copy(h2_rows[m][:, EARLY * CJ:LAST * CJ], products[m])
        products = quantise_and_multiply(LAST, round_on_vector(LAST), reused_bank("second"))
        nc.scalar.copy(h2_rows[0][:, LAST * CJ:], products[0])
        for m in range(1, M_TILES):
            nc.vector.tensor_copy(h2_rows[m][:, LAST * CJ:], products[m])

        for m in range(M_TILES):
            for u in range(2):
                at_n3 = new([P, HALF], F32, "at_n3_%d_%d" % (m, u))
                nc.scalar.activation(at_n3[:], h2_rows[m][:].indirect(entries(n3_sb, u * HALF, HALF)), COPY)
                gap = new([P, HALF], F32, "gap%d_%d" % (m, u))
                nc.vector.tensor_tensor(
                    gap[:], h2_rows[m][:].indirect(entries(n2_sb, u * HALF, HALF)), at_n3[:], ALU.subtract)
                nc.sync.dma_start(out[m * P:(m + 1) * P, u * HALF:(u + 1) * HALF], gap[:])
